import numpy as np, ml_dtypes
CORES = [40,41,42,43,44,45,46,47]
N = 8
import mx_ref
BF = ml_dtypes.bfloat16
def entries(a):
    return np.ascontiguousarray(a.T).reshape(-1)
def table(e):
    return np.ascontiguousarray(np.reshape(e, (-1, 16)).T).astype(np.int32)
def cols(t, e):
    v = np.concatenate([t.reshape(128, -1, 4), np.zeros((128, 1, 4), BF)], axis=1)
    return np.ascontiguousarray(v[:, e]).reshape(128, -1)
def pick(q, e):
    c = np.concatenate([q[0].reshape(128, -1, 4), np.zeros((128, 1, 4), np.uint8)], axis=1); s = np.concatenate([q[1], np.ones((16, 1), np.uint8)], axis=1)
    return (np.ascontiguousarray(c[:, e].reshape(128, -1)), np.ascontiguousarray(s[:, e]))
def join(*qs):
    return (np.concatenate([q[0] for q in qs], axis=1), np.concatenate([q[1] for q in qs], axis=1))
def put(q, e, v):
    c, s = q[0].reshape(128, -1, 4).copy(), q[1].copy(); c[:, e] = v[0].reshape(128, -1, 4); s[:, e] = v[1]
    return (c.reshape(128, -1), s)
def pk(c, s):
    return (np.ascontiguousarray(c), mx_ref.live(s))
def emit(q):
    return q[0], q[1]
def decode(q):
    o = []
    for b in range(4):
        e = np.zeros((128, 128, 4), np.float32); e[np.arange(128), np.arange(128), b] = 1
        o.append(mx_ref.matmul(mx_ref.quantize(e.reshape(128, 512).astype(BF)), q))
    return np.stack(o, axis=2).reshape(128, -1)
def f(rng, *shape):
    return mx_ref.flush((rng.standard_normal(shape, dtype=np.float32) * np.exp2(rng.integers(-2, 3, shape[:-1] + (1,)))).astype(BF))
def wide(rng, *shape, cols=0):
    v = rng.standard_normal(shape, dtype=np.float32) * np.exp2(rng.integers(-12, 13, shape)).astype(np.float32)
    if cols: v *= np.repeat(np.exp2(rng.integers(-cols, cols + 1, shape[:-2] + (1, shape[-1] // 4))) * (rng.random(shape[:-2] + (1, shape[-1] // 4)) > 0.0625), 4, axis=-1).astype(np.float32)
    return mx_ref.flush(v.astype(BF))
T, CAPP = 256, 64
def lists(rng, count, high=False, among=T, unnamed=0):
    sn, so = np.full((N, N * CAPP), -1), np.zeros((N, 512), int)
    for d in range(N):
        filled = []
        for s in range(N):
            c = np.sort(rng.permutation(CAPP)[:count[s, d]]); k = rng.permutation(among)[:c.size]
            sn[s, d * CAPP + c] = np.sort(k)[::-1] if high else k
            filled.append(s * CAPP + c)
        filled = np.concatenate(filled)
        if unnamed: filled = rng.permutation(filled)[unnamed:]
        o = np.concatenate([filled, rng.choice(filled, 512 - filled.size)])
        so[d] = np.sort(o)[::-1] if high else rng.permutation(o)
    return {"sn": np.stack([table(v) for v in sn]), "so": np.stack([table(v) for v in so])}
def setup_inputs(rng):
    return {"x": f(rng, N, 128, 4 * T), **lists(rng, rng.integers(1, CAPP + 1, (N, N)))}
def setup_inputs_full(rng):
    return {**setup_inputs(rng), **lists(rng, np.full((N, N), CAPP))}
def setup_inputs_one(rng):
    n = np.zeros((N, N), int); n[rng.integers(0, N)] = 3
    return {**setup_inputs(rng), **lists(rng, n, among=rng.permutation(T)[:3])}
def setup_inputs_own(rng):
    return {**setup_inputs(rng), **lists(rng, CAPP * np.eye(N, dtype=int))}
def setup_inputs_reversed(rng):
    return {**setup_inputs(rng), **lists(rng, rng.integers(1, CAPP + 1, (N, N)), high=True, unnamed=3)}
def setup_inputs_spread(rng):
    d = setup_inputs(rng); d["x"] = wide(rng, N, 128, 4 * T, cols=8); return d
def check_inputs(d):
    b = []
    a = np.stack([entries(d["sn"][s]) for s in range(N)])
    for r in range(N):
        pairs = [a[r, q * CAPP:q * CAPP + CAPP] for q in range(N)]
        if a[r].min() < -1 or a[r].max() >= T or any(len(set(g[g >= 0].tolist())) != (g >= 0).sum() for g in pairs): b.append("sn")
        e = entries(d["so"][r])
        if e.min() < 0 or e.max() >= N * CAPP: b.append("so")
        elif (a[e // CAPP, r * CAPP + e % CAPP] < 0).any(): b.append("so")
    return b
def reference(x, sn, so):
    v = np.concatenate([x[s] for s in range(N)], axis=1)
    a = np.stack([entries(sn[s]) for s in range(N)])
    fc, fs = np.zeros((N, 128, 2048), np.uint8), np.zeros((N, 16, 512), np.uint8)
    bc, bs = np.zeros((N, 128, 2048), np.uint8), np.zeros((N, 16, 512), np.uint8)
    for d in range(N):
        e = entries(so[d]); s = e // CAPP
        F = mx_ref.quantize(cols(v, s * T + a[s, d * CAPP + e % CAPP]))
        fc[d], fs[d] = emit(F)
        m = decode(F).reshape(128, 512, 4).transpose(0, 2, 1).reshape(512, 512)
        m = np.ascontiguousarray(m.T).astype(BF)
        bt = []
        for b in range(4):
            k = np.ascontiguousarray(m[:, 128 * b:128 * b + 128]).reshape(128, 4, 128)
            bt.append(mx_ref.quantize(np.ascontiguousarray(k.transpose(0, 2, 1)).reshape(128, 512)))
        bc[d], bs[d] = emit(join(*bt))
    return {"fc": fc, "fs": fs, "bc": bc, "bs": bs}

@@ -1,0 +1,171 @@
+from concourse.bass import DstId, RemoteDMATransfer
+from concourse.mybir import dt, AluOpType, ActivationFunctionType
+
+N, TOK, CAPP, PLACES = 8, 256, 64, 512
+PARTS = [(0, 384), (384, 512)]
+CHUNKS = [(0, 1), (1, 2), (2, 4)]
+
+F8 = "float8_e4m3fn_x4"
+SCRATCH = {
+    "xt": ("sbuf", [128, 4 * TOK], "bfloat16"),
+    "qx": ("sbuf", [128, TOK], F8), "sx": ("sbuf", [128, TOK], "uint8"),
+    "snl": ("sbuf", [128, 32], "int32"), "sno": ("sbuf", [128, 32], "uint16"),
+    "slotq": ("sbuf", [128, 512], F8), "slots": ("sbuf", [128, 512], "uint8"),
+    "landq": ("sbuf", [128, 512], F8), "lands": ("sbuf", [128, 512], "uint8"),
+    "dl": ("dram", [16, 132], "int32"), "pl": ("sbuf", [128, 128], "int32"), "po": ("sbuf", [128, 32], "uint16"),
+    "blkq": ("sbuf", [128, 512], F8), "blks": ("sbuf", [128, 512], "uint8"),
+    "fq": ("sbuf", [128, 512], F8), "fsc": ("sbuf", [128, 512], "uint8"),
+    "jrow": ("sbuf", [128, 512], "bfloat16"), "pcol": ("sbuf", [128, 1], "float32"),
+    "wcol": ("sbuf", [128, 1], "int32"), "vcol": ("sbuf", [128, 1], "int32"), "fcol": ("sbuf", [128, 1], "float32"),
+    "krow": ("sbuf", [128, 32], "int32"), "ko": ("sbuf", [128, 32], "uint16"),
+    "ident": ("sbuf", [128, 2048], "bfloat16"),
+    "iq": ("sbuf", [128, 512], F8), "is8": ("sbuf", [128, 512], "uint8"),
+    "ps0": ("psum", [128, 2048], "float32"), "ps1": ("psum", [128, 2048], "float32"),
+    "bt": ("sbuf", [128, 2048], "bfloat16"),
+    "bq": ("sbuf", [128, 512], F8), "bsc": ("sbuf", [128, 512], "uint8"),
+}
+SEMAPHORES = (["xin", "snin", "so1", "so2", "iot", "idb", "idq", "kv", "kf", "ko", "sno", "qx", "pickq", "picks",
+               "ownq", "owns", "po", "arrq", "arrs", "sent", "fq", "fsc", "st1", "st2"]
+              + ["bk%s%d" % (k, c) for k in "qs" for c in range(3)]
+              + ["mm%d%d" % (h, t) for h in range(2) for t in range(4)]
+              + ["bt0", "bt1", "bq0", "bq1"])
+
+
+def rank_program(g, core, T, topo):
+    rank = T.rank_of(core)
+    if rank is None:
+        return
+    S = T.sem
+    V, A, Y, E = g.vector, g.scalar, g.sync, g.tensor
+    COPY = ActivationFunctionType.Copy
+    OP = AluOpType
+
+    def words(view):
+        return view.bitcast(dt.uint32)
+
+    Y.dma_start(T.xt[:], T.x[:]).then_inc(S.xin, 16)
+    for k in range(8):
+        (A if k < 5 else Y).dma_start(T.snl[16 * k:16 * k + 16, :], T.sn[:]).then_inc(S.snin, 16)
+    for a in range(4):
+        Y.dma_start(T.dl[4 * a:4 * a + 4, 4 - a:132 - a], T.so[:]).then_inc(S.so1, 16)
+    Y.wait_ge(S.so1, 64)
+    for k in range(8):
+        Y.dma_start(T.pl[16 * k:16 * k + 16, 0:125], T.dl[:, 4:129]).then_inc(S.so2, 16)
+
+    g.iota(T.jrow[:], [[1, 512]], -256, 0, allow_small_or_imprecise_dtypes=True).then_inc(S.iot, 1)
+    g.iota(T.pcol[:], [[0, 1]], -256, 4, allow_small_or_imprecise_dtypes=True).then_inc(S.iot, 1)
+    g.iota(T.wcol[:], [[0, 1]], 0, 513).then_inc(S.iot, 1)
+    g.iota(T.krow[:], [[4, 32]], 0, 0).then_inc(S.iot, 1)
+    V.wait_ge(S.iot, 4)
+    for t in range(4):
+        V.tensor_scalar(T.ident[:, t:2048:4], T.jrow[:], float(t), T.pcol[:], OP.subtract, OP.is_equal).then_inc(S.idb, 1)
+
+    runs = [(lo, hi) for lo, hi in ((0, rank), (rank + 1, N)) if hi > lo]
+    V.wait_ge(S.snin, 128)
+    V.tensor_copy(T.sno[:], T.snl[:]).then_inc(S.sno, 1)
+    V.wait_ge(S.xin, 16)
+    V.quantize_mx(T.qx[:], T.sx[:], T.xt[:]).then_inc(S.qx, 1)
+    for q in (V, A):
+        q.wait_ge(S.sno, 1)
+        q.wait_ge(S.qx, 1)
+    for lo, hi in runs:
+        V.tensor_copy(words(T.slotq[:, 64 * lo:64 * hi]), words(T.qx[:]).indirect(T.sno[:, 4 * lo:4 * hi])).then_inc(S.pickq, 1)
+        A.activation(T.slots[:, 64 * lo:64 * hi], T.sx[:].indirect(T.sno[:, 4 * lo:4 * hi]), COPY).then_inc(S.picks, 1)
+    r0, r1 = 64 * rank, 64 * rank + 64
+    V.tensor_copy(words(T.landq[:, r0:r1]), words(T.qx[:]).indirect(T.sno[:, 4 * rank:4 * rank + 4])).then_inc(S.ownq, 1)
+    A.activation(T.lands[:, r0:r1], T.sx[:].indirect(T.sno[:, 4 * rank:4 * rank + 4]), COPY).then_inc(S.owns, 1)
+
+    near = [d for d in range(N) if d != rank and topo.die(T.cores[d]) == topo.die(core)]
+    far = [d for d in range(N) if topo.die(T.cores[d]) != topo.die(core)]
+    masks = {}
+    for first, group in ((0, far), (1, near)):
+        for i, d in enumerate(group):
+            e = topo.engines(core, T.cores[d])[first::2]
+            masks[d] = sum(1 << k for k in e[2 * i:2 * i + 2])
+
+    def put(src, dst, sem):
+        tr = []
+        for d in far + near:
+            rid, pid, _ = topo.addr(T.cores[d])
+            tr.append(RemoteDMATransfer(dst_ids=[DstId(rid=rid, pnc=pid)], dma_engine_mask=masks[d], remote_sem=sem,
+                                        srcs=[src(d)], dsts=[dst]))
+        g.remote_dma_fused(tr, local_sem=S.sent)
+
+    g.wait_ge(S.pickq, len(runs))
+    put(lambda d: T.slotq[:, 64 * d:64 * d + 64].bitcast(dt.uint8), T.landq[:, r0:r1].bitcast(dt.uint8), S.arrq)
+    g.wait_ge(S.picks, len(runs))
+    put(lambda d: T.slots[:, 64 * d:64 * d + 64], T.lands[:, r0:r1], S.arrs)
+    g.wait_ge(S.sent, 28)
+
+    V.wait_ge(S.idb, 4)
+    V.quantize_mx(T.iq[:], T.is8[:], T.ident[:]).then_inc(S.idq, 1)
+    V.tensor_scalar(T.vcol[:], T.wcol[:], 2, 387, OP.logical_shift_right, OP.bitwise_and).then_inc(S.kv, 1)
+    V.wait_ge(S.kv, 1)
+    V.tensor_copy(T.fcol[:], T.vcol[:]).then_inc(S.kf, 1)
+    V.wait_ge(S.kf, 1)
+    V.tensor_scalar(T.ko[:], T.krow[:], T.fcol[:], None, OP.add).then_inc(S.ko, 1)
+    V.wait_ge(S.so2, 128)
+    V.tensor_copy(T.po[:], T.pl[:, 0:125:4]).then_inc(S.po, 1)
+
+    V.wait_ge(S.ownq, 1)
+    V.wait_ge(S.po, 1)
+    V.wait_ge(S.arrq, 14)
+    A.wait_ge(S.owns, 1)
+    A.wait_ge(S.po, 1)
+    A.wait_ge(S.arrs, 14)
+    for c, (lo, hi) in enumerate(CHUNKS):
+        off = T.po[:, 8 * lo:8 * hi]
+        V.tensor_copy(words(T.blkq[:, 128 * lo:128 * hi]), words(T.landq[:]).indirect(off)).then_inc(S["bkq%d" % c], 1)
+        A.activation(T.blks[:, 128 * lo:128 * hi], T.lands[:].indirect(off), COPY).then_inc(S["bks%d" % c], 1)
+
+    E.wait_ge(S.idq, 1)
+    for h, (f0, f1) in enumerate(PARTS):
+        ps = T["ps%d" % h]
+        for t in range(4):
+            for c, (lo, hi) in enumerate(CHUNKS):
+                if h == 0 and lo == t:
+                    E.wait_ge(S["bkq%d" % c], 1)
+                    E.wait_ge(S["bks%d" % c], 1)
+            E.matmul_mx(ps[:, 512 * t:512 * t + f1 - f0], T.blkq[:, 128 * t:128 * t + 128], T.blks[:, 128 * t:128 * t + 128],
+                        T.iq[:, f0:f1], T.is8[:, f0:f1], True, True).then_inc(S["mm%d%d" % (h, t)], 1)
+
+    def turn(q, h, t):
+        f0, f1 = PARTS[h]
+        q.wait_ge(S["mm%d%d" % (h, t)], 1)
+        out, in_ = T.bt[:, 4 * f0 + t:4 * f1:4], T["ps%d" % h][:, 512 * t:512 * t + f1 - f0]
+        i = V.tensor_copy(out, in_) if q is V else A.activation(out, in_, COPY)
+        i.then_inc(S["bt%d" % h], 1)
+
+    def pack(h):
+        f0, f1 = PARTS[h]
+        V.wait_ge(S["bt%d" % h], 4)
+        V.quantize_mx(T.bq[:, f0:f1], T.bsc[:, f0:f1], T.bt[:, 4 * f0:4 * f1]).then_inc(S["bq%d" % h], 1)
+
+    turn(V, 0, 0)
+    for t in (1, 2, 3):
+        turn(A, 0, t)
+    for c in range(3):
+        V.wait_ge(S["bkq%d" % c], 1)
+        A.wait_ge(S["bks%d" % c], 1)
+    V.wait_ge(S.ko, 1)
+    V.tensor_copy(words(T.fq[:]), words(T.blkq[:]).indirect(T.ko[:])).then_inc(S.fq, 1)
+    pack(0)
+    for t in (0, 1, 2):
+        turn(A, 1, t)
+    turn(V, 1, 3)
+    pack(1)
+    A.wait_ge(S.ko, 1)
+    A.activation(T.fsc[:], T.blks[:].indirect(T.ko[:]), COPY).then_inc(S.fsc, 1)
+
+    Y.wait_ge(S.fq, 1)
+    Y.dma_start(T.fc[:], T.fq[:].bitcast(dt.uint8)).then_inc(S.st1, 16)
+    for h, (f0, f1) in enumerate(PARTS):
+        Y.wait_ge(S["bq%d" % h], 1)
+        Y.dma_start(T.bc[:, 4 * f0:4 * f1], T.bq[:, f0:f1].bitcast(dt.uint8)).then_inc(S.st1, 16)
+    for k in range(4):
+        Y.dma_start(T.bs[4 * k:4 * k + 4, :], T.bsc[32 * k:32 * k + 4, :]).then_inc(S.st1, 16)
+    Y.wait_ge(S.st1, 112)
+    A.wait_ge(S.fsc, 1)
+    for k in range(4):
+        A.dma_start(T.fs[4 * k:4 * k + 4, :], T.fsc[32 * k:32 * k + 4, :]).then_inc(S.st2, 16)
+    A.wait_ge(S.st2, 64)

@@ -2,7 +2,7 @@ from concourse.bass import DstId, RemoteDMATransfer
 from concourse.mybir import dt, AluOpType, ActivationFunctionType
 
 N, TOK, CAPP, PLACES = 8, 256, 64, 512
-PARTS = [(0, 384), (384, 512)]
+PARTS = [(0, 320), (320, 512)]
 CHUNKS = [(0, 1), (1, 2), (2, 4)]
 
 F8 = "float8_e4m3fn_x4"
@@ -24,8 +24,8 @@ SCRATCH = {
     "bt": ("sbuf", [128, 2048], "bfloat16"),
     "bq": ("sbuf", [128, 512], F8), "bsc": ("sbuf", [128, 512], "uint8"),
 }
-SEMAPHORES = (["xin", "snin", "so1", "so2", "iot", "idb", "idq", "kv", "kf", "ko", "sno", "qx", "pickq", "picks",
-               "ownq", "owns", "po", "arrq", "arrs", "sent", "fq", "fsc", "st1", "st2"]
+SEMAPHORES = (["xin", "snin", "so1", "so2", "iot", "iot2", "idb", "idq", "kv", "kf", "ko", "sno", "qx",
+               "pickf", "pickn", "picks", "ownq", "owns", "po", "arrq", "arrs", "sent", "fq0", "fq1", "fsc", "st1", "st2"]
               + ["bk%s%d" % (k, c) for k in "qs" for c in range(3)]
               + ["mm%d%d" % (h, t) for h in range(2) for t in range(4)]
               + ["bt0", "bt1", "bq0", "bq1"])
@@ -54,13 +54,23 @@ def rank_program(g, core, T, topo):
 
     g.iota(T.jrow[:], [[1, 512]], -256, 0, allow_small_or_imprecise_dtypes=True).then_inc(S.iot, 1)
     g.iota(T.pcol[:], [[0, 1]], -256, 4, allow_small_or_imprecise_dtypes=True).then_inc(S.iot, 1)
-    g.iota(T.wcol[:], [[0, 1]], 0, 513).then_inc(S.iot, 1)
-    g.iota(T.krow[:], [[4, 32]], 0, 0).then_inc(S.iot, 1)
-    V.wait_ge(S.iot, 4)
-    for t in range(4):
+    g.iota(T.wcol[:], [[0, 1]], 0, 513).then_inc(S.iot2, 1)
+    g.iota(T.krow[:], [[4, 32]], 0, 0).then_inc(S.iot2, 1)
+
+    def identity(t):
         V.tensor_scalar(T.ident[:, t:2048:4], T.jrow[:], float(t), T.pcol[:], OP.subtract, OP.is_equal).then_inc(S.idb, 1)
 
-    runs = [(lo, hi) for lo, hi in ((0, rank), (rank + 1, N)) if hi > lo]
+    V.wait_ge(S.iot, 2)
+    identity(0)
+    identity(1)
+
+    near = [d for d in range(N) if d != rank and topo.die(T.cores[d]) == topo.die(core)]
+    far = [d for d in range(N) if topo.die(T.cores[d]) != topo.die(core)]
+
+    def runs(group):
+        cut = [i for i in range(1, len(group)) if group[i] != group[i - 1] + 1]
+        return [(group[i], group[j - 1] + 1) for i, j in zip([0] + cut, cut + [len(group)])]
+
     V.wait_ge(S.snin, 128)
     V.tensor_copy(T.sno[:], T.snl[:]).then_inc(S.sno, 1)
     V.wait_ge(S.xin, 16)
@@ -68,37 +78,42 @@ def rank_program(g, core, T, topo):
     for q in (V, A):
         q.wait_ge(S.sno, 1)
         q.wait_ge(S.qx, 1)
-    for lo, hi in runs:
-        V.tensor_copy(words(T.slotq[:, 64 * lo:64 * hi]), words(T.qx[:]).indirect(T.sno[:, 4 * lo:4 * hi])).then_inc(S.pickq, 1)
-        A.activation(T.slots[:, 64 * lo:64 * hi], T.sx[:].indirect(T.sno[:, 4 * lo:4 * hi]), COPY).then_inc(S.picks, 1)
+    for group, sem in ((far, S.pickf), (near, S.pickn)):
+        for lo, hi in runs(group):
+            off = T.sno[:, 4 * lo:4 * hi]
+            V.tensor_copy(words(T.slotq[:, 64 * lo:64 * hi]), words(T.qx[:]).indirect(off)).then_inc(sem, 1)
+            A.activation(T.slots[:, 64 * lo:64 * hi], T.sx[:].indirect(off), COPY).then_inc(S.picks, 1)
     r0, r1 = 64 * rank, 64 * rank + 64
-    V.tensor_copy(words(T.landq[:, r0:r1]), words(T.qx[:]).indirect(T.sno[:, 4 * rank:4 * rank + 4])).then_inc(S.ownq, 1)
-    A.activation(T.lands[:, r0:r1], T.sx[:].indirect(T.sno[:, 4 * rank:4 * rank + 4]), COPY).then_inc(S.owns, 1)
+    off = T.sno[:, 4 * rank:4 * rank + 4]
+    V.tensor_copy(words(T.landq[:, r0:r1]), words(T.qx[:]).indirect(off)).then_inc(S.ownq, 1)
+    A.activation(T.lands[:, r0:r1], T.sx[:].indirect(off), COPY).then_inc(S.owns, 1)
 
-    near = [d for d in range(N) if d != rank and topo.die(T.cores[d]) == topo.die(core)]
-    far = [d for d in range(N) if topo.die(T.cores[d]) != topo.die(core)]
     masks = {}
     for first, group in ((0, far), (1, near)):
         for i, d in enumerate(group):
             e = topo.engines(core, T.cores[d])[first::2]
             masks[d] = sum(1 << k for k in e[2 * i:2 * i + 2])
 
-    def put(src, dst, sem):
+    def put(group, src, dst, sem):
         tr = []
-        for d in far + near:
+        for d in group:
             rid, pid, _ = topo.addr(T.cores[d])
             tr.append(RemoteDMATransfer(dst_ids=[DstId(rid=rid, pnc=pid)], dma_engine_mask=masks[d], remote_sem=sem,
                                         srcs=[src(d)], dsts=[dst]))
         g.remote_dma_fused(tr, local_sem=S.sent)
 
-    g.wait_ge(S.pickq, len(runs))
-    put(lambda d: T.slotq[:, 64 * d:64 * d + 64].bitcast(dt.uint8), T.landq[:, r0:r1].bitcast(dt.uint8), S.arrq)
-    g.wait_ge(S.picks, len(runs))
-    put(lambda d: T.slots[:, 64 * d:64 * d + 64], T.lands[:, r0:r1], S.arrs)
+    for group, sem in ((far, S.pickf), (near, S.pickn)):
+        g.wait_ge(sem, len(runs(group)))
+        put(group, lambda d: T.slotq[:, 64 * d:64 * d + 64].bitcast(dt.uint8), T.landq[:, r0:r1].bitcast(dt.uint8), S.arrq)
+    g.wait_ge(S.picks, len(runs(far)) + len(runs(near)))
+    put(far + near, lambda d: T.slots[:, 64 * d:64 * d + 64], T.lands[:, r0:r1], S.arrs)
     g.wait_ge(S.sent, 28)
 
+    identity(2)
+    identity(3)
     V.wait_ge(S.idb, 4)
     V.quantize_mx(T.iq[:], T.is8[:], T.ident[:]).then_inc(S.idq, 1)
+    V.wait_ge(S.iot2, 2)
     V.tensor_scalar(T.vcol[:], T.wcol[:], 2, 387, OP.logical_shift_right, OP.bitwise_and).then_inc(S.kv, 1)
     V.wait_ge(S.kv, 1)
     V.tensor_copy(T.fcol[:], T.vcol[:]).then_inc(S.kf, 1)
@@ -141,30 +156,33 @@ def rank_program(g, core, T, topo):
         V.wait_ge(S["bt%d" % h], 4)
         V.quantize_mx(T.bq[:, f0:f1], T.bsc[:, f0:f1], T.bt[:, 4 * f0:4 * f1]).then_inc(S["bq%d" % h], 1)
 
-    turn(V, 0, 0)
-    for t in (1, 2, 3):
-        turn(A, 0, t)
-    for c in range(3):
+    for c in range(len(CHUNKS)):
         V.wait_ge(S["bkq%d" % c], 1)
-        A.wait_ge(S["bks%d" % c], 1)
     V.wait_ge(S.ko, 1)
-    V.tensor_copy(words(T.fq[:]), words(T.blkq[:]).indirect(T.ko[:])).then_inc(S.fq, 1)
+    for k in range(2):
+        V.tensor_copy(words(T.fq[:, 256 * k:256 * k + 256]), words(T.blkq[:]).indirect(T.ko[:, 16 * k:16 * k + 16])).then_inc(S["fq%d" % k], 1)
+    for t in (0, 2, 3):
+        turn(A, 0, t)
+    turn(V, 0, 1)
     pack(0)
     for t in (0, 1, 2):
         turn(A, 1, t)
     turn(V, 1, 3)
     pack(1)
+    for c in range(len(CHUNKS)):
+        A.wait_ge(S["bks%d" % c], 1)
     A.wait_ge(S.ko, 1)
     A.activation(T.fsc[:], T.blks[:].indirect(T.ko[:]), COPY).then_inc(S.fsc, 1)
 
-    Y.wait_ge(S.fq, 1)
-    Y.dma_start(T.fc[:], T.fq[:].bitcast(dt.uint8)).then_inc(S.st1, 16)
+    for k in range(2):
+        Y.wait_ge(S["fq%d" % k], 1)
+        Y.dma_start(T.fc[:, 1024 * k:1024 * k + 1024], T.fq[:, 256 * k:256 * k + 256].bitcast(dt.uint8)).then_inc(S.st1, 16)
     for h, (f0, f1) in enumerate(PARTS):
         Y.wait_ge(S["bq%d" % h], 1)
         Y.dma_start(T.bc[:, 4 * f0:4 * f1], T.bq[:, f0:f1].bitcast(dt.uint8)).then_inc(S.st1, 16)
     for k in range(4):
         Y.dma_start(T.bs[4 * k:4 * k + 4, :], T.bsc[32 * k:32 * k + 4, :]).then_inc(S.st1, 16)
-    Y.wait_ge(S.st1, 112)
+    Y.wait_ge(S.st1, 128)
     A.wait_ge(S.fsc, 1)
     for k in range(4):
         A.dma_start(T.fs[4 * k:4 * k + 4, :], T.fsc[32 * k:32 * k + 4, :]).then_inc(S.st2, 16)

@@ -15,7 +15,7 @@ SCRATCH = {
     "dl": ("dram", [16, 132], "int32"), "pl": ("sbuf", [128, 128], "int32"), "po": ("sbuf", [128, 32], "uint16"),
     "blkq": ("sbuf", [128, 512], F8), "blks": ("sbuf", [128, 512], "uint8"),
     "fq": ("sbuf", [128, 512], F8), "fsc": ("sbuf", [128, 512], "uint8"),
-    "jrow": ("sbuf", [128, 512], "bfloat16"), "pcol": ("sbuf", [128, 1], "float32"),
+    "jrow": ("sbuf", [128, 128], "bfloat16"), "pcol": ("sbuf", [128, 1], "bfloat16"),
     "wcol": ("sbuf", [128, 1], "int32"), "vcol": ("sbuf", [128, 1], "int32"), "fcol": ("sbuf", [128, 1], "float32"),
     "krow": ("sbuf", [128, 32], "int32"), "ko": ("sbuf", [128, 32], "uint16"),
     "ident": ("sbuf", [128, 2048], "bfloat16"),
@@ -52,13 +52,15 @@ def rank_program(g, core, T, topo):
     for k in range(8):
         Y.dma_start(T.pl[16 * k:16 * k + 16, 0:125], T.dl[:, 4:129]).then_inc(S.so2, 16)
 
-    g.iota(T.jrow[:], [[1, 512]], -256, 0, allow_small_or_imprecise_dtypes=True).then_inc(S.iot, 1)
     g.iota(T.pcol[:], [[0, 1]], -256, 4, allow_small_or_imprecise_dtypes=True).then_inc(S.iot, 1)
+    g.iota(T.jrow[:], [[1, 128]], 0, 0, allow_small_or_imprecise_dtypes=True).then_inc(S.iot, 1)
     g.iota(T.wcol[:], [[0, 1]], 0, 513).then_inc(S.iot2, 1)
     g.iota(T.krow[:], [[4, 32]], 0, 0).then_inc(S.iot2, 1)
 
     def identity(t):
-        V.tensor_scalar(T.ident[:, t:2048:4], T.jrow[:], float(t), T.pcol[:], OP.subtract, OP.is_equal).then_inc(S.idb, 1)
+        for b in range(4):
+            V.tensor_scalar(T.ident[:, 512 * b + t:512 * b + 512:4], T.jrow[:], float(128 * b - t - 256), T.pcol[:],
+                            OP.add, OP.is_equal).then_inc(S.idb, 1)
 
     V.wait_ge(S.iot, 2)
     identity(0)
@@ -111,7 +113,7 @@ def rank_program(g, core, T, topo):
 
     identity(2)
     identity(3)
-    V.wait_ge(S.idb, 4)
+    V.wait_ge(S.idb, 16)
     V.quantize_mx(T.iq[:], T.is8[:], T.ident[:]).then_inc(S.idq, 1)
     V.wait_ge(S.iot2, 2)
     V.tensor_scalar(T.vcol[:], T.wcol[:], 2, 387, OP.logical_shift_right, OP.bitwise_and).then_inc(S.kv, 1)

@@ -25,10 +25,35 @@ SCRATCH = {
     "bq": ("sbuf", [128, 512], F8), "bsc": ("sbuf", [128, 512], "uint8"),
 }
 SEMAPHORES = (["xin", "snin", "so1", "so2", "iot", "iot2", "idb", "idq", "kv", "kf", "ko", "sno", "qx",
-               "pickf", "pickn", "picks", "ownq", "owns", "po", "arrq", "arrs", "sent", "fq0", "fq1", "fsc", "st1", "st2"]
+               "pick0", "pick1", "picks", "ownq", "owns", "po", "arrq", "arrs", "sent", "fq0", "fq1", "fsc", "st1", "st2"]
               + ["bk%s%d" % (k, c) for k in "qs" for c in range(3)]
               + ["mm%d%d" % (h, t) for h in range(2) for t in range(4)]
               + ["bt0", "bt1", "bq0", "bq1"])
+
+
+def runs(group):
+    group = sorted(group)
+    cut = [0] + [i for i in range(1, len(group)) if group[i] != group[i - 1] + 1] + [len(group)]
+    return [(group[i], group[j - 1] + 1) for i, j in zip(cut, cut[1:])]
+
+
+def peers(cores, s, topo):
+    near = [d for d in range(N) if d != s and topo.die(cores[d]) == topo.die(cores[s])]
+    far = [d for d in range(N) if topo.die(cores[d]) != topo.die(cores[s])]
+    first = min(far, key=lambda f: len(runs([d for d in near + far if d != f])))
+    return near, [first] + [d for d in far if d != first]
+
+
+def plan(cores, s, topo):
+    near, far = peers(cores, s, topo)
+    e = topo.engines(cores[s], cores[far[0]])
+    a, b = e[0::2], e[1::2]
+    return [
+        [(far[0], a[0:2])],
+        [(far[k], a[2 * k:2 * k + 2]) for k in (1, 2, 3)] + [(near[0], b[0:2]), (near[1], b[2:4]), (near[2], b[4:8])],
+        [(far[0], a[0:4]), (far[1], a[4:8]), (far[3], b[0:4]), (near[0], b[4:6]), (near[1], b[6:8])],
+        [(far[2], a), (near[2], b)],
+    ]
 
 
 def rank_program(g, core, T, topo):
@@ -66,13 +91,8 @@ def rank_program(g, core, T, topo):
     identity(0)
     identity(1)
 
-    near = [d for d in range(N) if d != rank and topo.die(T.cores[d]) == topo.die(core)]
-    far = [d for d in range(N) if topo.die(T.cores[d]) != topo.die(core)]
-
-    def runs(group):
-        cut = [i for i in range(1, len(group)) if group[i] != group[i - 1] + 1]
-        return [(group[i], group[j - 1] + 1) for i, j in zip([0] + cut, cut + [len(group)])]
-
+    near, far = peers(T.cores, rank, topo)
+    first, rest = [far[0]], near + far[1:]
     V.wait_ge(S.snin, 128)
     V.tensor_copy(T.sno[:], T.snl[:]).then_inc(S.sno, 1)
     V.wait_ge(S.xin, 16)
@@ -80,7 +100,7 @@ def rank_program(g, core, T, topo):
     for q in (V, A):
         q.wait_ge(S.sno, 1)
         q.wait_ge(S.qx, 1)
-    for group, sem in ((far, S.pickf), (near, S.pickn)):
+    for group, sem in ((first, S.pick0), (rest, S.pick1)):
         for lo, hi in runs(group):
             off = T.sno[:, 4 * lo:4 * hi]
             V.tensor_copy(words(T.slotq[:, 64 * lo:64 * hi]), words(T.qx[:]).indirect(off)).then_inc(sem, 1)
@@ -90,26 +110,30 @@ def rank_program(g, core, T, topo):
     V.tensor_copy(words(T.landq[:, r0:r1]), words(T.qx[:]).indirect(off)).then_inc(S.ownq, 1)
     A.activation(T.lands[:, r0:r1], T.sx[:].indirect(off), COPY).then_inc(S.owns, 1)
 
-    masks = {}
-    for first, group in ((0, far), (1, near)):
-        for i, d in enumerate(group):
-            e = topo.engines(core, T.cores[d])[first::2]
-            masks[d] = sum(1 << k for k in e[2 * i:2 * i + 2])
+    calls = [plan(T.cores, s, topo) for s in range(N)]
 
-    def put(group, src, dst, sem):
+    def engines(cs):
+        return sum(len(e) for c in cs for _, e in c)
+
+    def arriving(lo, hi):
+        return sum(len(e) for s in range(N) if s != rank for c in calls[s][lo:hi] for d, e in c if d == rank)
+
+    def put(call, src, dst, sem):
         tr = []
-        for d in group:
+        for d, e in call:
             rid, pid, _ = topo.addr(T.cores[d])
-            tr.append(RemoteDMATransfer(dst_ids=[DstId(rid=rid, pnc=pid)], dma_engine_mask=masks[d], remote_sem=sem,
-                                        srcs=[src(d)], dsts=[dst]))
+            tr.append(RemoteDMATransfer(dst_ids=[DstId(rid=rid, pnc=pid)], dma_engine_mask=sum(1 << k for k in e),
+                                        remote_sem=sem, srcs=[src(d)], dsts=[dst]))
         g.remote_dma_fused(tr, local_sem=S.sent)
 
-    for group, sem in ((far, S.pickf), (near, S.pickn)):
+    for k, sem, group in ((0, S.pick0, first), (1, S.pick1, rest)):
         g.wait_ge(sem, len(runs(group)))
-        put(group, lambda d: T.slotq[:, 64 * d:64 * d + 64].bitcast(dt.uint8), T.landq[:, r0:r1].bitcast(dt.uint8), S.arrq)
-    g.wait_ge(S.picks, len(runs(far)) + len(runs(near)))
-    put(far + near, lambda d: T.slots[:, 64 * d:64 * d + 64], T.lands[:, r0:r1], S.arrs)
-    g.wait_ge(S.sent, 28)
+        put(calls[rank][k], lambda d: T.slotq[:, 64 * d:64 * d + 64].bitcast(dt.uint8),
+            T.landq[:, r0:r1].bitcast(dt.uint8), S.arrq)
+    g.wait_ge(S.picks, len(runs(first)) + len(runs(rest)))
+    for k in (2, 3):
+        put(calls[rank][k], lambda d: T.slots[:, 64 * d:64 * d + 64], T.lands[:, r0:r1], S.arrs)
+    g.wait_ge(S.sent, engines(calls[rank]))
 
     identity(2)
     identity(3)
@@ -126,10 +150,10 @@ def rank_program(g, core, T, topo):
 
     V.wait_ge(S.ownq, 1)
     V.wait_ge(S.po, 1)
-    V.wait_ge(S.arrq, 14)
+    V.wait_ge(S.arrq, arriving(0, 2))
     A.wait_ge(S.owns, 1)
     A.wait_ge(S.po, 1)
-    A.wait_ge(S.arrs, 14)
+    A.wait_ge(S.arrs, arriving(2, 4))
     for c, (lo, hi) in enumerate(CHUNKS):
         off = T.po[:, 8 * lo:8 * hi]
         V.tensor_copy(words(T.blkq[:, 128 * lo:128 * hi]), words(T.landq[:]).indirect(off)).then_inc(S["bkq%d" % c], 1)
@@ -163,14 +187,13 @@ def rank_program(g, core, T, topo):
     V.wait_ge(S.ko, 1)
     for k in range(2):
         V.tensor_copy(words(T.fq[:, 256 * k:256 * k + 256]), words(T.blkq[:]).indirect(T.ko[:, 16 * k:16 * k + 16])).then_inc(S["fq%d" % k], 1)
-    for t in (0, 2, 3):
-        turn(A, 0, t)
-    turn(V, 0, 1)
+    turn(V, 0, 3)
     pack(0)
-    for t in (0, 1, 2):
-        turn(A, 1, t)
+    turn(V, 1, 2)
     turn(V, 1, 3)
     pack(1)
+    for h, t in ((0, 0), (0, 1), (0, 2), (1, 0), (1, 1)):
+        turn(A, h, t)
     for c in range(len(CHUNKS)):
         A.wait_ge(S["bks%d" % c], 1)
     A.wait_ge(S.ko, 1)

from concourse.bass import DstId, RemoteDMATransfer
from concourse.mybir import dt, AluOpType, ActivationFunctionType

N, TOK, CAPP, PLACES = 8, 256, 64, 512
PARTS = [(0, 320), (320, 512)]
CHUNKS = [(0, 1), (1, 2), (2, 4)]

F8 = "float8_e4m3fn_x4"
SCRATCH = {
    "xt": ("sbuf", [128, 4 * TOK], "bfloat16"),
    "qx": ("sbuf", [128, TOK], F8), "sx": ("sbuf", [128, TOK], "uint8"),
    "snl": ("sbuf", [128, 32], "int32"), "sno": ("sbuf", [128, 32], "uint16"),
    "slotq": ("sbuf", [128, 512], F8), "slots": ("sbuf", [128, 512], "uint8"),
    "landq": ("sbuf", [128, 512], F8), "lands": ("sbuf", [128, 512], "uint8"),
    "dl": ("dram", [16, 132], "int32"), "pl": ("sbuf", [128, 128], "int32"), "po": ("sbuf", [128, 32], "uint16"),
    "blkq": ("sbuf", [128, 512], F8), "blks": ("sbuf", [128, 512], "uint8"),
    "fq": ("sbuf", [128, 512], F8), "fsc": ("sbuf", [128, 512], "uint8"),
    "jrow": ("sbuf", [128, 128], "bfloat16"), "pcol": ("sbuf", [128, 1], "bfloat16"),
    "wcol": ("sbuf", [128, 1], "int32"), "vcol": ("sbuf", [128, 1], "int32"), "fcol": ("sbuf", [128, 1], "float32"),
    "krow": ("sbuf", [128, 32], "int32"), "ko": ("sbuf", [128, 32], "uint16"),
    "ident": ("sbuf", [128, 2048], "bfloat16"),
    "iq": ("sbuf", [128, 512], F8), "is8": ("sbuf", [128, 512], "uint8"),
    "ps0": ("psum", [128, 2048], "float32"), "ps1": ("psum", [128, 2048], "float32"),
    "bt": ("sbuf", [128, 2048], "bfloat16"),
    "bq": ("sbuf", [128, 512], F8), "bsc": ("sbuf", [128, 512], "uint8"),
}
SEMAPHORES = (["xin", "snin", "so1", "so2", "iot", "iot2", "idb", "idq", "kv", "kf", "ko", "sno", "qx",
               "pick0", "pick1", "picks", "ownq", "owns", "po", "arrq", "arrs", "sent", "fq0", "fq1", "fsc", "st1", "st2"]
              + ["bk%s%d" % (k, c) for k in "qs" for c in range(3)]
              + ["mm%d%d" % (h, t) for h in range(2) for t in range(4)]
              + ["bt0", "bt1", "bq0", "bq1"])


def runs(group):
    group = sorted(group)
    cut = [0] + [i for i in range(1, len(group)) if group[i] != group[i - 1] + 1] + [len(group)]
    return [(group[i], group[j - 1] + 1) for i, j in zip(cut, cut[1:])]


def peers(cores, s, topo):
    near = [d for d in range(N) if d != s and topo.die(cores[d]) == topo.die(cores[s])]
    far = [d for d in range(N) if topo.die(cores[d]) != topo.die(cores[s])]
    first = min(far, key=lambda f: len(runs([d for d in near + far if d != f])))
    return near, [first] + [d for d in far if d != first]


def plan(cores, s, topo):
    near, far = peers(cores, s, topo)
    e = topo.engines(cores[s], cores[far[0]])
    a, b = e[0::2], e[1::2]
    return [
        [(far[0], a[0:2])],
        [(far[k], a[2 * k:2 * k + 2]) for k in (1, 2, 3)] + [(near[0], b[0:2]), (near[1], b[2:4]), (near[2], b[4:8])],
        [(far[0], a[0:4]), (far[1], a[4:8]), (far[3], b[0:4]), (near[0], b[4:6]), (near[1], b[6:8])],
        [(far[2], a), (near[2], b)],
    ]


def rank_program(g, core, T, topo):
    rank = T.rank_of(core)
    if rank is None:
        return
    S = T.sem
    V, A, Y, E = g.vector, g.scalar, g.sync, g.tensor
    COPY = ActivationFunctionType.Copy
    OP = AluOpType

    def words(view):
        return view.bitcast(dt.uint32)

    Y.dma_start(T.xt[:], T.x[:]).then_inc(S.xin, 16)
    for k in range(8):
        (A if k < 5 else Y).dma_start(T.snl[16 * k:16 * k + 16, :], T.sn[:]).then_inc(S.snin, 16)
    for a in range(4):
        Y.dma_start(T.dl[4 * a:4 * a + 4, 4 - a:132 - a], T.so[:]).then_inc(S.so1, 16)
    Y.wait_ge(S.so1, 64)
    for k in range(8):
        Y.dma_start(T.pl[16 * k:16 * k + 16, 0:125], T.dl[:, 4:129]).then_inc(S.so2, 16)

    g.iota(T.pcol[:], [[0, 1]], -256, 4, allow_small_or_imprecise_dtypes=True).then_inc(S.iot, 1)
    g.iota(T.jrow[:], [[1, 128]], 0, 0, allow_small_or_imprecise_dtypes=True).then_inc(S.iot, 1)
    g.iota(T.wcol[:], [[0, 1]], 0, 513).then_inc(S.iot2, 1)
    g.iota(T.krow[:], [[4, 32]], 0, 0).then_inc(S.iot2, 1)

    def identity(t):
        for b in range(4):
            V.tensor_scalar(T.ident[:, 512 * b + t:512 * b + 512:4], T.jrow[:], float(128 * b - t - 256), T.pcol[:],
                            OP.add, OP.is_equal).then_inc(S.idb, 1)

    V.wait_ge(S.iot, 2)
    identity(0)
    identity(1)

    near, far = peers(T.cores, rank, topo)
    first, rest = [far[0]], near + far[1:]
    V.wait_ge(S.snin, 128)
    V.tensor_copy(T.sno[:], T.snl[:]).then_inc(S.sno, 1)
    V.wait_ge(S.xin, 16)
    V.quantize_mx(T.qx[:], T.sx[:], T.xt[:]).then_inc(S.qx, 1)
    for q in (V, A):
        q.wait_ge(S.sno, 1)
        q.wait_ge(S.qx, 1)
    for group, sem in ((first, S.pick0), (rest, S.pick1)):
        for lo, hi in runs(group):
            off = T.sno[:, 4 * lo:4 * hi]
            V.tensor_copy(words(T.slotq[:, 64 * lo:64 * hi]), words(T.qx[:]).indirect(off)).then_inc(sem, 1)
            A.activation(T.slots[:, 64 * lo:64 * hi], T.sx[:].indirect(off), COPY).then_inc(S.picks, 1)
    r0, r1 = 64 * rank, 64 * rank + 64
    off = T.sno[:, 4 * rank:4 * rank + 4]
    V.tensor_copy(words(T.landq[:, r0:r1]), words(T.qx[:]).indirect(off)).then_inc(S.ownq, 1)
    A.activation(T.lands[:, r0:r1], T.sx[:].indirect(off), COPY).then_inc(S.owns, 1)

    calls = [plan(T.cores, s, topo) for s in range(N)]

    def engines(cs):
        return sum(len(e) for c in cs for _, e in c)

    def arriving(lo, hi):
        return sum(len(e) for s in range(N) if s != rank for c in calls[s][lo:hi] for d, e in c if d == rank)

    def put(call, src, dst, sem):
        tr = []
        for d, e in call:
            rid, pid, _ = topo.addr(T.cores[d])
            tr.append(RemoteDMATransfer(dst_ids=[DstId(rid=rid, pnc=pid)], dma_engine_mask=sum(1 << k for k in e),
                                        remote_sem=sem, srcs=[src(d)], dsts=[dst]))
        g.remote_dma_fused(tr, local_sem=S.sent)

    for k, sem, group in ((0, S.pick0, first), (1, S.pick1, rest)):
        g.wait_ge(sem, len(runs(group)))
        put(calls[rank][k], lambda d: T.slotq[:, 64 * d:64 * d + 64].bitcast(dt.uint8),
            T.landq[:, r0:r1].bitcast(dt.uint8), S.arrq)
    g.wait_ge(S.picks, len(runs(first)) + len(runs(rest)))
    for k in (2, 3):
        put(calls[rank][k], lambda d: T.slots[:, 64 * d:64 * d + 64], T.lands[:, r0:r1], S.arrs)
    g.wait_ge(S.sent, engines(calls[rank]))

    identity(2)
    identity(3)
    V.wait_ge(S.idb, 16)
    V.quantize_mx(T.iq[:], T.is8[:], T.ident[:]).then_inc(S.idq, 1)
    V.wait_ge(S.iot2, 2)
    V.tensor_scalar(T.vcol[:], T.wcol[:], 2, 387, OP.logical_shift_right, OP.bitwise_and).then_inc(S.kv, 1)
    V.wait_ge(S.kv, 1)
    V.tensor_copy(T.fcol[:], T.vcol[:]).then_inc(S.kf, 1)
    V.wait_ge(S.kf, 1)
    V.tensor_scalar(T.ko[:], T.krow[:], T.fcol[:], None, OP.add).then_inc(S.ko, 1)
    V.wait_ge(S.so2, 128)
    V.tensor_copy(T.po[:], T.pl[:, 0:125:4]).then_inc(S.po, 1)

    V.wait_ge(S.ownq, 1)
    V.wait_ge(S.po, 1)
    V.wait_ge(S.arrq, arriving(0, 2))
    A.wait_ge(S.owns, 1)
    A.wait_ge(S.po, 1)
    A.wait_ge(S.arrs, arriving(2, 4))
    for c, (lo, hi) in enumerate(CHUNKS):
        off = T.po[:, 8 * lo:8 * hi]
        V.tensor_copy(words(T.blkq[:, 128 * lo:128 * hi]), words(T.landq[:]).indirect(off)).then_inc(S["bkq%d" % c], 1)
        A.activation(T.blks[:, 128 * lo:128 * hi], T.lands[:].indirect(off), COPY).then_inc(S["bks%d" % c], 1)

    E.wait_ge(S.idq, 1)
    for h, (f0, f1) in enumerate(PARTS):
        ps = T["ps%d" % h]
        for t in range(4):
            for c, (lo, hi) in enumerate(CHUNKS):
                if h == 0 and lo == t:
                    E.wait_ge(S["bkq%d" % c], 1)
                    E.wait_ge(S["bks%d" % c], 1)
            E.matmul_mx(ps[:, 512 * t:512 * t + f1 - f0], T.blkq[:, 128 * t:128 * t + 128], T.blks[:, 128 * t:128 * t + 128],
                        T.iq[:, f0:f1], T.is8[:, f0:f1], True, True).then_inc(S["mm%d%d" % (h, t)], 1)

    def turn(q, h, t):
        f0, f1 = PARTS[h]
        q.wait_ge(S["mm%d%d" % (h, t)], 1)
        out, in_ = T.bt[:, 4 * f0 + t:4 * f1:4], T["ps%d" % h][:, 512 * t:512 * t + f1 - f0]
        i = V.tensor_copy(out, in_) if q is V else A.activation(out, in_, COPY)
        i.then_inc(S["bt%d" % h], 1)

    def pack(h):
        f0, f1 = PARTS[h]
        V.wait_ge(S["bt%d" % h], 4)
        V.quantize_mx(T.bq[:, f0:f1], T.bsc[:, f0:f1], T.bt[:, 4 * f0:4 * f1]).then_inc(S["bq%d" % h], 1)

    for c in range(len(CHUNKS)):
        V.wait_ge(S["bkq%d" % c], 1)
    V.wait_ge(S.ko, 1)
    for k in range(2):
        V.tensor_copy(words(T.fq[:, 256 * k:256 * k + 256]), words(T.blkq[:]).indirect(T.ko[:, 16 * k:16 * k + 16])).then_inc(S["fq%d" % k], 1)
    turn(V, 0, 3)
    pack(0)
    turn(V, 1, 2)
    turn(V, 1, 3)
    pack(1)
    for h, t in ((0, 0), (0, 1), (0, 2), (1, 0), (1, 1)):
        turn(A, h, t)
    for c in range(len(CHUNKS)):
        A.wait_ge(S["bks%d" % c], 1)
    A.wait_ge(S.ko, 1)
    A.activation(T.fsc[:], T.blks[:].indirect(T.ko[:]), COPY).then_inc(S.fsc, 1)

    for k in range(2):
        Y.wait_ge(S["fq%d" % k], 1)
        Y.dma_start(T.fc[:, 1024 * k:1024 * k + 1024], T.fq[:, 256 * k:256 * k + 256].bitcast(dt.uint8)).then_inc(S.st1, 16)
    for h, (f0, f1) in enumerate(PARTS):
        Y.wait_ge(S["bq%d" % h], 1)
        Y.dma_start(T.bc[:, 4 * f0:4 * f1], T.bq[:, f0:f1].bitcast(dt.uint8)).then_inc(S.st1, 16)
    for k in range(4):
        Y.dma_start(T.bs[4 * k:4 * k + 4, :], T.bsc[32 * k:32 * k + 4, :]).then_inc(S.st1, 16)
    Y.wait_ge(S.st1, 128)
    A.wait_ge(S.fsc, 1)
    for k in range(4):
        A.dma_start(T.fs[4 * k:4 * k + 4, :], T.fsc[32 * k:32 * k + 4, :]).then_inc(S.st2, 16)
    A.wait_ge(S.st2, 64)
